import numpy as np, ml_dtypes
CORES = [66,70,74,78,82,86,90,94,98,102,106,110,114,118,122,126]
N = 16
NP, NBK, TK, CAP = 8, 2, 256, 3
DEST = [[14,9],[10,15],[13,9],[8,10],[9,11],[14,13],[10,15],[11,12]]
def setup_inputs(rng):
    return {"x": rng.standard_normal((N, 128, NBK * TK), dtype=np.float32).astype(ml_dtypes.bfloat16), "w": (rng.standard_normal((N, 128, 128), dtype=np.float32) / 8).astype(ml_dtypes.bfloat16)}
def setup_inputs_big(rng):
    d = setup_inputs(rng)
    for k in ("x", "w"): d[k] = (d[k].astype(np.float32) * 1024.0).astype(d[k].dtype)
    return d
def setup_inputs_small(rng):
    d = setup_inputs(rng)
    for k in ("x", "w"): d[k] = (d[k].astype(np.float32) * (1 / 1024.0)).astype(d[k].dtype)
    return d
def setup_inputs_apart(rng):
    d = setup_inputs(rng)
    f = (10.0 ** rng.permutation(np.linspace(-1.5, 1.5, N))).astype(np.float32).reshape(N, 1, 1)
    for k in ("x", "w"): d[k] = (d[k].astype(np.float32) * f).astype(d[k].dtype)
    return d
def reference(x, w):
    X, W = x.astype(np.float64), w.astype(np.float64)
    y = np.full((N, 128, CAP * TK), np.nan); n = [0] * N
    for p in range(NP):
        for c in range(NBK):
            q = DEST[p][c]
            y[q][:, TK * n[q]:TK * n[q] + TK] = W[q].T @ np.maximum(W[p].T @ X[p][:, TK * c:TK * c + TK], 0.0)
            n[q] += 1
    return {"y": y.astype(ml_dtypes.bfloat16 if x.dtype != np.float64 else np.float64)}

@@ -1,0 +1,126 @@
+from concourse.mybir import AluOpType
+
+NP = 8
+NBK = 2
+TK = 256
+CAP = 3
+SIM_CORES = 128
+
+SCRATCH = {
+    "wt": ("sbuf", [128, 128], "bfloat16"),
+    "x0": ("sbuf", [128, TK], "bfloat16"),
+    "x1": ("sbuf", [128, TK], "bfloat16"),
+    "zero": ("sbuf", [128, TK], "float32"),
+    "h0": ("sbuf", [128, TK], "bfloat16"),
+    "h1": ("sbuf", [128, TK], "bfloat16"),
+    "land0": ("sbuf", [128, TK], "bfloat16"),
+    "land1": ("sbuf", [128, TK], "bfloat16"),
+    "land2": ("sbuf", [128, TK], "bfloat16"),
+    "out0": ("sbuf", [128, TK], "bfloat16"),
+    "out1": ("sbuf", [128, TK], "bfloat16"),
+    "out2": ("sbuf", [128, TK], "bfloat16"),
+    "ps0": ("psum", [128, 512], "float32"),
+    "ps1": ("psum", [128, 512], "float32"),
+    "ps2": ("psum", [128, 512], "float32"),
+}
+SEMAPHORES = ["lw", "lx0", "lx1", "zs", "mm0", "mm1", "mm2", "ev0", "ev1", "ev2",
+              "arr0", "arr1", "arr2", "st0", "st1", "st2", "sent"]
+
+
+def way(topo, src, dst):
+    cs, cd, d = topo.chip(src), topo.chip(dst), topo.die(src)
+    if cs == cd:
+        return []
+    if topo.same_plane(cs, cd):
+        return [("out", cs, d), ("in", cd, d)]
+    if topo.mates(cs, cd):
+        return [("mate", cs, d)]
+    mate = [k for k in sorted({topo.chip(c) for c in range(SIM_CORES)}) if topo.mates(cs, k)][0]
+    return [("mate", cs, d), ("out", mate, d), ("in", cd, d)]
+
+
+def plan_order(topo, cores, dest):
+    uses = {}
+    for p in range(NP):
+        for c in range(NBK):
+            q = dest[p][c]
+            uses[(p, c)] = [(l, 4) for l in way(topo, cores[p], cores[q])] + [(("core", q), 1)]
+    best = None
+    for code in range(NBK ** NP):
+        first = [(code >> p) & 1 for p in range(NP)]
+        load = {}
+        for (p, c), ls in uses.items():
+            wave = 0 if c == first[p] else 1
+            for l, wt in ls:
+                n, _ = load.get((l, wave), (0, wt))
+                load[(l, wave)] = (n + 1, wt)
+        cost = sum(n * n * wt * (2 + wave) for (l, wave), (n, wt) in load.items())
+        if best is None or cost < best[0]:
+            best = (cost, first)
+    return best[1]
+
+
+def rank_program(g, core, T, topo):
+    rank = T.rank_of(core)
+    if rank is None:
+        return
+    dest = T.tables["DEST"]
+    cores = T.cores
+    sem = T.sem
+    first = plan_order(topo, cores, dest)
+    slot, owned = {}, {}
+    for p in range(NP):
+        for c in range(NBK):
+            lst = owned.setdefault(dest[p][c], [])
+            slot[(p, c)] = len(lst)
+            lst.append((p, c))
+
+    def engines(src, dst):
+        m = topo.mask(src, dst)
+        return m, bin(m).count("1")
+
+    if rank < NP:
+        blocks = [first[rank], 1 - first[rank]]
+        g.sync.dma_start(T.wt[:], T.w[:]).then_inc(sem.lw, 16)
+        for i, c in enumerate(blocks):
+            qd = g.scalar if i == 0 else g.sync
+            qd.dma_start(T["x%d" % i][:], T.x[:, c * TK:(c + 1) * TK]).then_inc(sem["lx%d" % i], 16)
+        g.vector.memset(T.zero[:], 0.0).then_inc(sem.zs, 1)
+        g.vector.wait_ge(sem.zs, 1)
+        g.tensor.wait_ge(sem.lw, 16)
+        total = 0
+        for i, c in enumerate(blocks):
+            ps = T["ps%d" % i][:, 0:TK]
+            h = T["h%d" % i]
+            g.tensor.wait_ge(sem["lx%d" % i], 16)
+            g.tensor.matmul(ps, T.wt[:], T["x%d" % i][:], True, True).then_inc(sem["mm%d" % i], 1)
+            g.vector.wait_ge(sem["mm%d" % i], 1)
+            g.vector.tensor_tensor(h[:], ps, T.zero[:], AluOpType.max).then_inc(sem["ev%d" % i], 1)
+            dst = cores[dest[rank][c]]
+            k = slot[(rank, c)]
+            rid, pid, _ = topo.addr(dst)
+            m, n = engines(core, dst)
+            g.wait_ge(sem["ev%d" % i], 1)
+            g.remote_dma(T["land%d" % k][:], h[:], sem["arr%d" % k], sem.sent, pid, rid, m)
+            total += n
+        g.wait_ge(sem.sent, total)
+        return
+
+    mine = owned.get(rank, [])
+    g.sync.dma_start(T.wt[:], T.w[:]).then_inc(sem.lw, 16)
+    g.tensor.wait_ge(sem.lw, 16)
+    todo = sorted(mine, key=lambda pc: (0 if pc[1] == first[pc[0]] else 1, slot[pc]))
+    for i, (p, c) in enumerate(todo):
+        k = slot[(p, c)]
+        ps = T["ps%d" % k][:, 0:TK]
+        o = T["out%d" % k]
+        _, n = engines(cores[p], core)
+        g.tensor.wait_ge(sem["arr%d" % k], n)
+        g.tensor.matmul(ps, T.wt[:], T["land%d" % k][:], True, True).then_inc(sem["mm%d" % k], 1)
+        g.vector.wait_ge(sem["mm%d" % k], 1)
+        g.vector.tensor_copy(o[:], ps).then_inc(sem["ev%d" % k], 1)
+        qd = g.scalar if i % 2 == 0 else g.sync
+        qd.wait_ge(sem["ev%d" % k], 1)
+        qd.dma_start(T.y[:, k * TK:(k + 1) * TK], o[:]).then_inc(sem["st%d" % k], 16)
+    for (p, c) in todo:
+        g.wait_ge(sem["st%d" % slot[(p, c)]], 16)

@@ -4,7 +4,9 @@ NP = 8
 NBK = 2
 TK = 256
 CAP = 3
+HEAD = 64
 SIM_CORES = 128
+CUTS = [[(0, HEAD), (HEAD, TK - HEAD)], [(0, TK // 2), (TK // 2, TK // 2)]]
 
 SCRATCH = {
     "wt": ("sbuf", [128, 128], "bfloat16"),
@@ -19,12 +21,11 @@ SCRATCH = {
     "out0": ("sbuf", [128, TK], "bfloat16"),
     "out1": ("sbuf", [128, TK], "bfloat16"),
     "out2": ("sbuf", [128, TK], "bfloat16"),
-    "ps0": ("psum", [128, 512], "float32"),
-    "ps1": ("psum", [128, 512], "float32"),
-    "ps2": ("psum", [128, 512], "float32"),
 }
-SEMAPHORES = ["lw", "lx0", "lx1", "zs", "mm0", "mm1", "mm2", "ev0", "ev1", "ev2",
-              "arr0", "arr1", "arr2", "st0", "st1", "st2", "sent"]
+SEMAPHORES = ["lw", "lx0", "lx1", "lx2", "zs", "sent"]
+for _k in range(2 * CAP):
+    SCRATCH["ps%d" % _k] = ("psum", [128, 512], "float32")
+    SEMAPHORES += ["mm%d" % _k, "ev%d" % _k, "arr%d" % _k, "st%d" % _k]
 
 
 def way(topo, src, dst):
@@ -81,46 +82,62 @@ def rank_program(g, core, T, topo):
 
     if rank < NP:
         blocks = [first[rank], 1 - first[rank]]
+        c0, c1 = blocks[0] * TK, blocks[1] * TK
         g.sync.dma_start(T.wt[:], T.w[:]).then_inc(sem.lw, 16)
-        for i, c in enumerate(blocks):
-            qd = g.scalar if i == 0 else g.sync
-            qd.dma_start(T["x%d" % i][:], T.x[:, c * TK:(c + 1) * TK]).then_inc(sem["lx%d" % i], 16)
+        g.scalar.dma_start(T.x0[:, 0:HEAD], T.x[:, c0:c0 + HEAD]).then_inc(sem.lx0, 16)
+        g.sync.dma_start(T.x0[:, HEAD:TK], T.x[:, c0 + HEAD:c0 + TK]).then_inc(sem.lx1, 16)
+        g.scalar.dma_start(T.x1[:], T.x[:, c1:c1 + TK]).then_inc(sem.lx2, 16)
         g.vector.memset(T.zero[:], 0.0).then_inc(sem.zs, 1)
         g.vector.wait_ge(sem.zs, 1)
         g.tensor.wait_ge(sem.lw, 16)
+        work = [(0, 0, HEAD, sem.lx0), (0, HEAD, TK - HEAD, sem.lx1), (1, 0, TK, sem.lx2)]
+        for j, (i, a, wd, ld) in enumerate(work):
+            ps = T["ps%d" % j][:, 0:wd]
+            g.tensor.wait_ge(ld, 16)
+            g.tensor.matmul(ps, T.wt[:], T["x%d" % i][:, a:a + wd], True, True).then_inc(sem["mm%d" % j], 1)
+            g.vector.wait_ge(sem["mm%d" % j], 1)
+            g.vector.tensor_tensor(T["h%d" % i][:, a:a + wd], ps, T.zero[:, 0:wd],
+                                   AluOpType.max).then_inc(sem["ev%d" % j], 1)
         total = 0
         for i, c in enumerate(blocks):
-            ps = T["ps%d" % i][:, 0:TK]
-            h = T["h%d" % i]
-            g.tensor.wait_ge(sem["lx%d" % i], 16)
-            g.tensor.matmul(ps, T.wt[:], T["x%d" % i][:], True, True).then_inc(sem["mm%d" % i], 1)
-            g.vector.wait_ge(sem["mm%d" % i], 1)
-            g.vector.tensor_tensor(h[:], ps, T.zero[:], AluOpType.max).then_inc(sem["ev%d" % i], 1)
             dst = cores[dest[rank][c]]
             k = slot[(rank, c)]
             rid, pid, _ = topo.addr(dst)
             m, n = engines(core, dst)
-            g.wait_ge(sem["ev%d" % i], 1)
-            g.remote_dma(T["land%d" % k][:], h[:], sem["arr%d" % k], sem.sent, pid, rid, m)
-            total += n
+            for j, (a, wd) in enumerate(CUTS[i]):
+                if i == 0 or j == 0:
+                    g.wait_ge(sem["ev%d" % (j if i == 0 else 2)], 1)
+                g.remote_dma(T["land%d" % k][:, a:a + wd], T["h%d" % i][:, a:a + wd], sem["arr%d" % (2 * k + j)],
+                             sem.sent, pid, rid, m)
+                total += n
         g.wait_ge(sem.sent, total)
         return
 
     mine = owned.get(rank, [])
     g.sync.dma_start(T.wt[:], T.w[:]).then_inc(sem.lw, 16)
     g.tensor.wait_ge(sem.lw, 16)
-    todo = sorted(mine, key=lambda pc: (0 if pc[1] == first[pc[0]] else 1, slot[pc]))
-    for i, (p, c) in enumerate(todo):
+    units = []
+    for (p, c) in mine:
         k = slot[(p, c)]
-        ps = T["ps%d" % k][:, 0:TK]
-        o = T["out%d" % k]
+        hops = len(way(topo, cores[p], core))
+        if c == first[p]:
+            units.append((0, 0, hops, k, 0, TK, [2 * k, 2 * k + 1], p))
+        else:
+            for j, (a, wd) in enumerate(CUTS[1]):
+                units.append((1, j, hops, k, a, wd, [2 * k + j], p))
+    units.sort()
+    for i, (wave, j, hops, k, a, wd, arrs, p) in enumerate(units):
+        u = 2 * k + j
+        ps = T["ps%d" % u][:, 0:wd]
+        o = T["out%d" % k][:, a:a + wd]
         _, n = engines(cores[p], core)
-        g.tensor.wait_ge(sem["arr%d" % k], n)
-        g.tensor.matmul(ps, T.wt[:], T["land%d" % k][:], True, True).then_inc(sem["mm%d" % k], 1)
-        g.vector.wait_ge(sem["mm%d" % k], 1)
-        g.vector.tensor_copy(o[:], ps).then_inc(sem["ev%d" % k], 1)
-        qd = g.scalar if i % 2 == 0 else g.sync
-        qd.wait_ge(sem["ev%d" % k], 1)
-        qd.dma_start(T.y[:, k * TK:(k + 1) * TK], o[:]).then_inc(sem["st%d" % k], 16)
-    for (p, c) in todo:
-        g.wait_ge(sem["st%d" % slot[(p, c)]], 16)
+        for s in arrs:
+            g.tensor.wait_ge(sem["arr%d" % s], n)
+        g.tensor.matmul(ps, T.wt[:], T["land%d" % k][:, a:a + wd], True, True).then_inc(sem["mm%d" % u], 1)
+        g.vector.wait_ge(sem["mm%d" % u], 1)
+        g.vector.tensor_copy(o, ps).then_inc(sem["ev%d" % u], 1)
+        qd = g.sync if i % 2 == 0 else g.scalar
+        qd.wait_ge(sem["ev%d" % u], 1)
+        qd.dma_start(T.y[:, k * TK + a:k * TK + a + wd], o).then_inc(sem["st%d" % u], 16)
+    for (wave, j, hops, k, a, wd, arrs, p) in units:
+        g.wait_ge(sem["st%d" % (2 * k + j)], 16)

from concourse.mybir import AluOpType

NP = 8
NBK = 2
TK = 256
CAP = 3
HEAD = 64
SIM_CORES = 128
CUTS = [[(0, HEAD), (HEAD, TK - HEAD)], [(0, TK // 2), (TK // 2, TK // 2)]]

SCRATCH = {
    "wt": ("sbuf", [128, 128], "bfloat16"),
    "x0": ("sbuf", [128, TK], "bfloat16"),
    "x1": ("sbuf", [128, TK], "bfloat16"),
    "zero": ("sbuf", [128, TK], "float32"),
    "h0": ("sbuf", [128, TK], "bfloat16"),
    "h1": ("sbuf", [128, TK], "bfloat16"),
    "land0": ("sbuf", [128, TK], "bfloat16"),
    "land1": ("sbuf", [128, TK], "bfloat16"),
    "land2": ("sbuf", [128, TK], "bfloat16"),
    "out0": ("sbuf", [128, TK], "bfloat16"),
    "out1": ("sbuf", [128, TK], "bfloat16"),
    "out2": ("sbuf", [128, TK], "bfloat16"),
}
SEMAPHORES = ["lw", "lx0", "lx1", "lx2", "zs", "sent"]
for _k in range(2 * CAP):
    SCRATCH["ps%d" % _k] = ("psum", [128, 512], "float32")
    SEMAPHORES += ["mm%d" % _k, "ev%d" % _k, "arr%d" % _k, "st%d" % _k]


def way(topo, src, dst):
    cs, cd, d = topo.chip(src), topo.chip(dst), topo.die(src)
    if cs == cd:
        return []
    if topo.same_plane(cs, cd):
        return [("out", cs, d), ("in", cd, d)]
    if topo.mates(cs, cd):
        return [("mate", cs, d)]
    mate = [k for k in sorted({topo.chip(c) for c in range(SIM_CORES)}) if topo.mates(cs, k)][0]
    return [("mate", cs, d), ("out", mate, d), ("in", cd, d)]


def plan_order(topo, cores, dest):
    uses = {}
    for p in range(NP):
        for c in range(NBK):
            q = dest[p][c]
            uses[(p, c)] = [(l, 4) for l in way(topo, cores[p], cores[q])] + [(("core", q), 1)]
    best = None
    for code in range(NBK ** NP):
        first = [(code >> p) & 1 for p in range(NP)]
        load = {}
        for (p, c), ls in uses.items():
            wave = 0 if c == first[p] else 1
            for l, wt in ls:
                n, _ = load.get((l, wave), (0, wt))
                load[(l, wave)] = (n + 1, wt)
        cost = sum(n * n * wt * (2 + wave) for (l, wave), (n, wt) in load.items())
        if best is None or cost < best[0]:
            best = (cost, first)
    return best[1]


def rank_program(g, core, T, topo):
    rank = T.rank_of(core)
    if rank is None:
        return
    dest = T.tables["DEST"]
    cores = T.cores
    sem = T.sem
    first = plan_order(topo, cores, dest)
    slot, owned = {}, {}
    for p in range(NP):
        for c in range(NBK):
            lst = owned.setdefault(dest[p][c], [])
            slot[(p, c)] = len(lst)
            lst.append((p, c))

    def engines(src, dst):
        m = topo.mask(src, dst)
        return m, bin(m).count("1")

    if rank < NP:
        blocks = [first[rank], 1 - first[rank]]
        c0, c1 = blocks[0] * TK, blocks[1] * TK
        g.sync.dma_start(T.wt[:], T.w[:]).then_inc(sem.lw, 16)
        g.scalar.dma_start(T.x0[:, 0:HEAD], T.x[:, c0:c0 + HEAD]).then_inc(sem.lx0, 16)
        g.sync.dma_start(T.x0[:, HEAD:TK], T.x[:, c0 + HEAD:c0 + TK]).then_inc(sem.lx1, 16)
        g.scalar.dma_start(T.x1[:], T.x[:, c1:c1 + TK]).then_inc(sem.lx2, 16)
        g.vector.memset(T.zero[:], 0.0).then_inc(sem.zs, 1)
        g.vector.wait_ge(sem.zs, 1)
        g.tensor.wait_ge(sem.lw, 16)
        work = [(0, 0, HEAD, sem.lx0), (0, HEAD, TK - HEAD, sem.lx1), (1, 0, TK, sem.lx2)]
        for j, (i, a, wd, ld) in enumerate(work):
            ps = T["ps%d" % j][:, 0:wd]
            g.tensor.wait_ge(ld, 16)
            g.tensor.matmul(ps, T.wt[:], T["x%d" % i][:, a:a + wd], True, True).then_inc(sem["mm%d" % j], 1)
            g.vector.wait_ge(sem["mm%d" % j], 1)
            g.vector.tensor_tensor(T["h%d" % i][:, a:a + wd], ps, T.zero[:, 0:wd],
                                   AluOpType.max).then_inc(sem["ev%d" % j], 1)
        total = 0
        for i, c in enumerate(blocks):
            dst = cores[dest[rank][c]]
            k = slot[(rank, c)]
            rid, pid, _ = topo.addr(dst)
            m, n = engines(core, dst)
            for j, (a, wd) in enumerate(CUTS[i]):
                if i == 0 or j == 0:
                    g.wait_ge(sem["ev%d" % (j if i == 0 else 2)], 1)
                g.remote_dma(T["land%d" % k][:, a:a + wd], T["h%d" % i][:, a:a + wd], sem["arr%d" % (2 * k + j)],
                             sem.sent, pid, rid, m)
                total += n
        g.wait_ge(sem.sent, total)
        return

    mine = owned.get(rank, [])
    g.sync.dma_start(T.wt[:], T.w[:]).then_inc(sem.lw, 16)
    g.tensor.wait_ge(sem.lw, 16)
    units = []
    for (p, c) in mine:
        k = slot[(p, c)]
        hops = len(way(topo, cores[p], core))
        if c == first[p]:
            units.append((0, 0, hops, k, 0, TK, [2 * k, 2 * k + 1], p))
        else:
            for j, (a, wd) in enumerate(CUTS[1]):
                units.append((1, j, hops, k, a, wd, [2 * k + j], p))
    units.sort()
    for i, (wave, j, hops, k, a, wd, arrs, p) in enumerate(units):
        u = 2 * k + j
        ps = T["ps%d" % u][:, 0:wd]
        o = T["out%d" % k][:, a:a + wd]
        _, n = engines(cores[p], core)
        for s in arrs:
            g.tensor.wait_ge(sem["arr%d" % s], n)
        g.tensor.matmul(ps, T.wt[:], T["land%d" % k][:, a:a + wd], True, True).then_inc(sem["mm%d" % u], 1)
        g.vector.wait_ge(sem["mm%d" % u], 1)
        g.vector.tensor_copy(o, ps).then_inc(sem["ev%d" % u], 1)
        qd = g.sync if i % 2 == 0 else g.scalar
        qd.wait_ge(sem["ev%d" % u], 1)
        qd.dma_start(T.y[:, k * TK + a:k * TK + a + wd], o).then_inc(sem["st%d" % u], 16)
    for (wave, j, hops, k, a, wd, arrs, p) in units:
        g.wait_ge(sem["st%d" % (2 * k + j)], 16)
